import numpy as np
import ml_dtypes


def mxq(x, axis, fmt="e4m3"):
    dtype, down = {"e4m3": (ml_dtypes.float8_e4m3fn, 7), "e5m2": (ml_dtypes.float8_e5m2, 14)}[fmt]
    v = np.moveaxis(np.asarray(x, np.float32).astype(ml_dtypes.bfloat16).astype(np.float64), axis, -1)
    blocks = v.reshape(v.shape[:-1] + (-1, 32))
    amax = np.abs(blocks).max(-1, keepdims=True)
    byte = np.maximum(np.where(amax > 0, np.frexp(amax)[1] - 1 + 127, 0) - down, 1)
    scale = np.exp2(byte - 127.0)
    codes = (blocks / scale).astype(np.float32).astype(dtype).astype(np.float64)
    return np.moveaxis((codes * scale).reshape(v.shape), -1, axis)


WIDE = False


def mx_kscale(k):
    if not WIDE:
        return np.ones(k)
    levels = np.array([10, -10, 5, -5, 0])
    if k % 512:
        return np.exp2(np.random.permutation(np.resize(levels, k // 32))).repeat(32)
    a = np.empty((k // 512, 16))
    for p in range(k // 512):
        a[p, :8] = np.random.permutation(np.resize(levels, 8))
        for g in range(8):
            far = levels[np.abs(levels - a[p, g]) >= 10]
            a[p, g + 8] = far[np.random.randint(len(far))]
    return np.exp2(a.ravel()).repeat(32)


BF16 = ml_dtypes.bfloat16


def bf(x):
    return np.asarray(x, np.float32).astype(BF16)


def f64(x):
    return np.asarray(x).astype(np.float64)

def planes(Y):
    n, m = Y.shape
    b = f64(bf(Y)).reshape(n // 32, 32, m)
    amax = np.abs(b).max(1)
    byte = np.clip(np.where(amax > 0, np.frexp(amax)[1] - 1 + 127 - 7, 1), 1, 254)
    codes = (b * np.exp2(127.0 - byte)[:, None, :]).reshape(n, m).astype(np.float32).astype(ml_dtypes.float8_e4m3fn).view(np.uint8)
    words = codes.reshape(n // 512, 128, 4, m).transpose(0, 1, 3, 2)
    return np.ascontiguousarray(words), np.ascontiguousarray(byte.astype(np.uint8).reshape(n // 512, 16, m))


B, N = 16, 512


def tanh_slope(z):
    th = np.tanh(z)
    return 1.0 - th * th


def setup_inputs():
    s = mx_kscale(N)
    return {
        "h": bf(np.random.standard_normal((B, N)) * s[None, :]),
        "xp": bf(0.5 * np.random.standard_normal((B, N))),
        "u": bf(np.random.standard_normal((N, N)) / np.sqrt(N) / s[:, None]),
        "a": bf(np.random.standard_normal((B, N, N)) * s[None, :, None]),
        "c1": bf(np.random.uniform(0.5, 1.0, (B,))),
        "c2": bf(np.random.uniform(2.0, 4.0, (B,))),
    }


def core(h, xp, u, a, c1, c2):
    h, xp, u, a, c1, c2 = f64(h), f64(xp), f64(u), f64(a), f64(c1), f64(c2)
    n = u.shape[0]
    z = np.sum(h[:, :, None] * u[None, :, :], axis=1) + xp
    d = tanh_slope(z)
    uq = mxq(u, 0, "e4m3")
    aq = mxq(a, 1, "e4m3")
    m = uq.T @ aq
    idx = np.arange(n)
    on_diag = (idx[:, None] == idx[None, :])[None, :, :]
    scaled = c1[:, None, None] * m
    t = np.where(on_diag, scaled + c2[:, None, None], scaled)
    return d[:, :, None] * t


def reference(h, xp, u, a, c1, c2):
    R_out = core(h, xp, u, a, c1, c2)
    words, scales = planes(np.moveaxis(R_out, 2, 0).reshape(512, -1))
    return R_out, words, scales

@@ -1,0 +1,223 @@
+from contextlib import ExitStack
+
+import concourse.mybir as mybir
+from concourse.masks import make_identity
+
+F32 = mybir.dt.float32
+BF16 = mybir.dt.bfloat16
+U32 = mybir.dt.uint32
+I32 = mybir.dt.int32
+U8 = mybir.dt.uint8
+FP8X4 = mybir.dt.float8_e4m3fn_x4
+ALU = mybir.AluOpType
+ACT = mybir.ActivationFunctionType
+
+B, N = 16, 512
+P = 128
+T = 4
+FLOPS = 2 * B * N * N * N + 2 * B * N * N
+
+AHEAD = 8
+GROUP = 4
+
+V_COLS = ((0, 128), (0, 256), (256, 512), (384, 512))
+S_COLS = ((128, 512), (256, 512), (0, 256), (0, 384))
+
+
+def tile_kroneckerfactoredrtrlinfluence_x1_kernel(tc, h, xp, u, a, c1, c2, out_0, out_1, out_2):
+    nc = tc.nc
+    with ExitStack() as ctx:
+        keep = ctx.enter_context(tc.tile_pool(name="keep", bufs=1))
+        raws = ctx.enter_context(tc.tile_pool(name="raws", bufs=AHEAD + 1))
+        stage = ctx.enter_context(tc.tile_pool(name="stage", bufs=3))
+        outs = ctx.enter_context(tc.tile_pool(name="outs", bufs=5))
+        psum = ctx.enter_context(tc.psum_pool(name="psum", bufs=1))
+        ctx.enter_context(tc.manual_schedule())
+
+        raw, grp, codes, scl = {}, {}, {}, {}
+        acc, o32, pbf, pcodes, pscl = {}, {}, {}, {}, {}
+
+        u_raw = keep.tile([P, T, N], BF16, name="u_raw", align_bytes=64)
+        nc.sync.dma_start(out=u_raw[:], in_=u.rearrange("(p j) i -> p j i", j=T))
+
+        def load(b):
+            raw[b] = raws.tile([P, T, N], BF16, name="a_raw", align_bytes=64)
+            nc.sync.dma_start(out=raw[b][:], in_=a[b].rearrange("(p j) l -> p j l", j=T))
+
+        for b in range(AHEAD):
+            load(b)
+
+        ident = keep.tile([P, P], F32, name="ident")
+        make_identity(nc, ident[:])
+        identb = keep.tile([P, P], BF16, name="identb")
+        make_identity(nc, identb[:])
+
+        hx = keep.tile([P, 2, N], BF16, name="hx", align_bytes=64)
+        nc.vector.memset(hx[:], 0.0)
+        nc.scalar.dma_start(out=hx[0:B, 0, :], in_=h)
+        nc.scalar.dma_start(out=hx[0:B, 1, :], in_=xp)
+        c1t = keep.tile([P, B], BF16, name="c1t", align_bytes=64)
+        c2t = keep.tile([P, B], BF16, name="c2t", align_bytes=64)
+        nc.scalar.dma_start(out=c1t[:], in_=c1.partition_broadcast(P))
+        nc.scalar.dma_start(out=c2t[:], in_=c2.partition_broadcast(P))
+
+        dg = []
+        for par in range(2):
+            tiles = []
+            for it in range(T):
+                w = V_COLS[it][1] - V_COLS[it][0]
+                d = keep.tile([P, w], F32, name="dg%d%d" % (par, it), align_bytes=64)
+                off = it * P - V_COLS[it][0]
+                if off > 0:
+                    nc.vector.memset(d[:, 0:off], 0.0)
+                if off + P < w:
+                    nc.vector.memset(d[:, off + P : w], 0.0)
+                tiles.append((d, off))
+            dg.append(tiles)
+
+        def interleave(src, dst):
+            nc.vector.tensor_copy(
+                out=dst[:].rearrange("p (c i) t -> p c t i", i=4),
+                in_=src[:].rearrange("p t (c i) -> p c t i", i=4),
+            )
+
+        def quantize(src, cw, sc):
+            nc.vector.quantize_mx(out=cw.bitcast(FP8X4), scales=sc, in_=src[:].rearrange("p n t -> p (n t)"))
+
+        u_grp = keep.tile([P, N, T], BF16, name="u_grp", align_bytes=64)
+        u_codes = keep.tile([P, N], U32, name="u_codes", align_bytes=64)
+        u_scl = keep.tile([P, N], U8, name="u_scl", align_bytes=64)
+
+        def interleave_a(b):
+            grp[b] = stage.tile([P, N, T], BF16, name="a_grp", align_bytes=64)
+            interleave(raw.pop(b), grp[b])
+
+        def quantize_a(b):
+            codes[b] = stage.tile([P, N], U32, name="a_codes", align_bytes=64)
+            scl[b] = stage.tile([P, N], U8, name="a_scl", align_bytes=64)
+            quantize(grp.pop(b), codes[b][:], scl[b][:])
+
+        hT_ps = psum.tile([P, T, P], BF16, name="hT_ps", tag="tp1")
+        for j in range(T):
+            nc.tensor.transpose(hT_ps[:, j, :], hx[:, 0, j:N:T], identb[:])
+        hT = keep.tile([P, T, B], BF16, name="hT", align_bytes=64)
+        nc.scalar.copy(out=hT[:], in_=hT_ps[:, :, 0:B])
+        z_ps = psum.tile([P, T, B], F32, name="z_ps", tag="tp0")
+        for it in range(T):
+            cols = slice(it * P, (it + 1) * P)
+            nc.tensor.matmul(z_ps[:, it, :], lhsT=hx[:, 1, cols], rhs=identb[:, 0:B], start=True, stop=False)
+            for j in range(T):
+                nc.tensor.matmul(z_ps[:, it, :], lhsT=u_raw[:, j, cols], rhs=hT[:, j, :], start=False, stop=(j == T - 1))
+        interleave(u_raw, u_grp)
+        interleave_a(0)
+        th = keep.tile([P, T, B], F32, name="th", align_bytes=64)
+        nc.scalar.activation(out=th[:], in_=z_ps[:], func=ACT.Tanh)
+        nth2 = keep.tile([P, T, B], F32, name="nth2", align_bytes=64)
+        nc.vector.scalar_tensor_tensor(out=nth2[:], in0=th[:], scalar=-1.0, in1=th[:], op0=ALU.mult, op1=ALU.mult)
+        quantize(u_grp, u_codes[:], u_scl[:])
+        dc1 = keep.tile([P, T, B], F32, name="dc1", align_bytes=64)
+        dc2 = keep.tile([P, T, B], F32, name="dc2", align_bytes=64)
+        for dst, c in ((dc1, c1t), (dc2, c2t)):
+            nc.vector.scalar_tensor_tensor(
+                out=dst[:], in0=nth2[:], scalar=1.0, in1=c[:].unsqueeze(1).to_broadcast([P, T, B]),
+                op0=ALU.add, op1=ALU.mult,
+            )
+
+        def diag(b):
+            for it in range(T):
+                d, off = dg[b % 2][it]
+                nc.vector.tensor_scalar(
+                    out=d[:, off : off + P], in0=ident[:], scalar1=dc2[:, it, b : b + 1], scalar2=None, op0=ALU.mult
+                )
+
+        def multiply(b):
+            acc[b] = []
+            for it in range(T):
+                ps = psum.tile([P, N], F32, name="mx%d" % it, tag="mx%d" % it)
+                nc.tensor.matmul_mx(
+                    out=ps[:],
+                    lhsT=u_codes[:, it * P : (it + 1) * P].bitcast(FP8X4),
+                    lhsT_scale=u_scl[:, it * P : (it + 1) * P],
+                    rhs=codes[b][:].bitcast(FP8X4),
+                    rhs_scale=scl[b][:],
+                    start=True,
+                    stop=True,
+                )
+                acc[b].append(ps)
+
+        def empty(b):
+            o32[b] = outs.tile([P, T, N], F32, name="o32", align_bytes=64)
+
+            def on_vector(it):
+                c0, cend = V_COLS[it]
+                nc.vector.scalar_tensor_tensor(
+                    out=o32[b][:, it, c0:cend], in0=acc[b][it][:, c0:cend], scalar=dc1[:, it, b : b + 1],
+                    in1=dg[b % 2][it][0][:], op0=ALU.mult, op1=ALU.add,
+                )
+
+            def on_scalar(it):
+                c0, cend = S_COLS[it]
+                nc.scalar.activation(
+                    out=o32[b][:, it, c0:cend], in_=acc[b][it][:, c0:cend], func=ACT.Copy, scale=dc1[:, it, b : b + 1]
+                )
+
+            for i0, i1 in ((0, 1), (2, 3)):
+                on_vector(i0)
+                on_scalar(i1)
+                on_vector(i1)
+                on_scalar(i0)
+
+        def turn(b):
+            pbf[b] = stage.tile([P, N, T], BF16, name="pbf", align_bytes=64)
+            for it in range(T):
+                tp = psum.tile([P, T, P], F32, name="tp%d" % it, tag="tp%d" % it)
+                for t in range(T):
+                    nc.tensor.transpose(tp[:, t, :], o32[b][:, it, t:N:T], ident[:])
+                nc.scalar.copy(out=pbf[b][:, it * P : (it + 1) * P, :], in_=tp[:].rearrange("p t i -> p i t"))
+
+        def quantize_p(b):
+            g = b // GROUP
+            if b % GROUP == 0:
+                pscl[g] = keep.tile([P, GROUP * N], U8, name="pscl%d" % g, align_bytes=64)
+            pcodes[b] = stage.tile([P, N], U32, name="pcodes", align_bytes=64)
+            k = b % GROUP
+            quantize(pbf.pop(b), pcodes[b][:], pscl[g][:, k * N : (k + 1) * N])
+
+        def store_o(b):
+            nc.sync.dma_start(out=out_0[b].rearrange("(t p) l -> p t l", p=P), in_=o32[b][:])
+
+        def store_p(b):
+            nc.sync.dma_start(
+                out=out_1[0, :, b * N : (b + 1) * N, :].rearrange("p m t -> p (m t)").bitcast(I32),
+                in_=pcodes[b][:].bitcast(I32),
+            )
+            if b % GROUP == GROUP - 1:
+                g = b // GROUP
+                for q in range(4):
+                    nc.sync.dma_start(
+                        out=out_2[0, 4 * q : 4 * q + 4, g * GROUP * N : (g + 1) * GROUP * N].bitcast(I32),
+                        in_=pscl[g][32 * q : 32 * q + 4, :].bitcast(I32),
+                    )
+
+        quantize_a(0)
+        diag(0)
+        interleave_a(1)
+        for s in range(B + 2):
+            if s + AHEAD < B:
+                load(s + AHEAD)
+            if s < B:
+                multiply(s)
+                empty(s)
+            if 1 <= s <= B:
+                turn(s - 1)
+            if s + 1 < B:
+                quantize_a(s + 1)
+                diag(s + 1)
+            if s + 2 < B:
+                interleave_a(s + 2)
+            if s >= 2:
+                quantize_p(s - 2)
+            if s < B:
+                store_o(s)
+            if s >= 2:
+                store_p(s - 2)

@@ -22,6 +22,9 @@ GROUP = 4
 
 V_COLS = ((0, 128), (0, 256), (256, 512), (384, 512))
 S_COLS = ((128, 512), (256, 512), (0, 256), (0, 384))
+WORDS = (1, 3)
+S_SHARE = 64
+S_SHARE_HEAD = 192
 
 
 def tile_kroneckerfactoredrtrlinfluence_x1_kernel(tc, h, xp, u, a, c1, c2, out_0, out_1, out_2):
@@ -35,8 +38,13 @@ def tile_kroneckerfactoredrtrlinfluence_x1_kernel(tc, h, xp, u, a, c1, c2, out_0
         ctx.enter_context(tc.manual_schedule())
 
         raw, grp, codes, scl = {}, {}, {}, {}
-        acc, o32, pbf, pcodes, pscl = {}, {}, {}, {}, {}
+        acc, o32, words, pbf, pcodes, pscl = {}, {}, {}, {}, {}, {}
 
+        hz = keep.tile([P, N], BF16, name="hz", align_bytes=64)
+        nc.vector.memset(hz[:], 0.0)
+        xz = keep.tile([P, N], BF16, name="xz", align_bytes=64)
+        nc.gpsimd.memset(xz[:], 0.0)
+        nc.scalar.dma_start(out=hz[0:B, :], in_=h)
         u_raw = keep.tile([P, T, N], BF16, name="u_raw", align_bytes=64)
         nc.sync.dma_start(out=u_raw[:], in_=u.rearrange("(p j) i -> p j i", j=T))
 
@@ -47,15 +55,11 @@ def tile_kroneckerfactoredrtrlinfluence_x1_kernel(tc, h, xp, u, a, c1, c2, out_0
         for b in range(AHEAD):
             load(b)
 
-        ident = keep.tile([P, P], F32, name="ident")
-        make_identity(nc, ident[:])
         identb = keep.tile([P, P], BF16, name="identb")
         make_identity(nc, identb[:])
-
-        hx = keep.tile([P, 2, N], BF16, name="hx", align_bytes=64)
-        nc.vector.memset(hx[:], 0.0)
-        nc.scalar.dma_start(out=hx[0:B, 0, :], in_=h)
-        nc.scalar.dma_start(out=hx[0:B, 1, :], in_=xp)
+        ident = keep.tile([P, P], F32, name="ident")
+        make_identity(nc, ident[:])
+        nc.scalar.dma_start(out=xz[0:B, :], in_=xp)
         c1t = keep.tile([P, B], BF16, name="c1t", align_bytes=64)
         c2t = keep.tile([P, B], BF16, name="c2t", align_bytes=64)
         nc.scalar.dma_start(out=c1t[:], in_=c1.partition_broadcast(P))
@@ -75,49 +79,53 @@ def tile_kroneckerfactoredrtrlinfluence_x1_kernel(tc, h, xp, u, a, c1, c2, out_0
                 tiles.append((d, off))
             dg.append(tiles)
 
-        def interleave(src, dst):
-            nc.vector.tensor_copy(
-                out=dst[:].rearrange("p (c i) t -> p c t i", i=4),
-                in_=src[:].rearrange("p t (c i) -> p c t i", i=4),
-            )
+        def interleave(src, dst, share):
+            cut = N - share
+            for eng, cols in ((nc.vector.tensor_copy, slice(0, cut)), (nc.scalar.copy, slice(cut, N))):
+                eng(
+                    out=dst[:, cols, :].rearrange("p (c i) t -> p c t i", i=4),
+                    in_=src[:, :, cols].rearrange("p t (c i) -> p c t i", i=4),
+                )
 
         def quantize(src, cw, sc):
-            nc.vector.quantize_mx(out=cw.bitcast(FP8X4), scales=sc, in_=src[:].rearrange("p n t -> p (n t)"))
+            nc.vector.quantize_mx(out=cw.bitcast(FP8X4), scales=sc, in_=src.rearrange("p n t -> p (n t)"))
 
         u_grp = keep.tile([P, N, T], BF16, name="u_grp", align_bytes=64)
         u_codes = keep.tile([P, N], U32, name="u_codes", align_bytes=64)
         u_scl = keep.tile([P, N], U8, name="u_scl", align_bytes=64)
 
-        def interleave_a(b):
+        def interleave_a(b, share=S_SHARE):
             grp[b] = stage.tile([P, N, T], BF16, name="a_grp", align_bytes=64)
-            interleave(raw.pop(b), grp[b])
+            interleave(raw.pop(b), grp[b], share)
 
         def quantize_a(b):
             codes[b] = stage.tile([P, N], U32, name="a_codes", align_bytes=64)
             scl[b] = stage.tile([P, N], U8, name="a_scl", align_bytes=64)
-            quantize(grp.pop(b), codes[b][:], scl[b][:])
+            quantize(grp.pop(b)[:], codes[b][:], scl[b][:])
 
         hT_ps = psum.tile([P, T, P], BF16, name="hT_ps", tag="tp1")
         for j in range(T):
-            nc.tensor.transpose(hT_ps[:, j, :], hx[:, 0, j:N:T], identb[:])
+            nc.tensor.transpose(hT_ps[:, j, :], hz[:, j:N:T], identb[:])
         hT = keep.tile([P, T, B], BF16, name="hT", align_bytes=64)
         nc.scalar.copy(out=hT[:], in_=hT_ps[:, :, 0:B])
         z_ps = psum.tile([P, T, B], F32, name="z_ps", tag="tp0")
         for it in range(T):
             cols = slice(it * P, (it + 1) * P)
-            nc.tensor.matmul(z_ps[:, it, :], lhsT=hx[:, 1, cols], rhs=identb[:, 0:B], start=True, stop=False)
+            nc.tensor.matmul(z_ps[:, it, :], lhsT=xz[:, cols], rhs=identb[:, 0:B], start=True, stop=False)
             for j in range(T):
                 nc.tensor.matmul(z_ps[:, it, :], lhsT=u_raw[:, j, cols], rhs=hT[:, j, :], start=False, stop=(j == T - 1))
-        interleave(u_raw, u_grp)
-        interleave_a(0)
+        interleave(u_raw, u_grp, S_SHARE_HEAD)
+        interleave_a(0, S_SHARE_HEAD)
         th = keep.tile([P, T, B], F32, name="th", align_bytes=64)
         nc.scalar.activation(out=th[:], in_=z_ps[:], func=ACT.Tanh)
+        quantize(u_grp[:], u_codes[:], u_scl[:])
+        quantize_a(0)
+        interleave_a(1)
         nth2 = keep.tile([P, T, B], F32, name="nth2", align_bytes=64)
         nc.vector.scalar_tensor_tensor(out=nth2[:], in0=th[:], scalar=-1.0, in1=th[:], op0=ALU.mult, op1=ALU.mult)
-        quantize(u_grp, u_codes[:], u_scl[:])
         dc1 = keep.tile([P, T, B], F32, name="dc1", align_bytes=64)
         dc2 = keep.tile([P, T, B], F32, name="dc2", align_bytes=64)
-        for dst, c in ((dc1, c1t), (dc2, c2t)):
+        for dst, c in ((dc2, c2t), (dc1, c1t)):
             nc.vector.scalar_tensor_tensor(
                 out=dst[:], in0=nth2[:], scalar=1.0, in1=c[:].unsqueeze(1).to_broadcast([P, T, B]),
                 op0=ALU.add, op1=ALU.mult,
@@ -126,13 +134,13 @@ def tile_kroneckerfactoredrtrlinfluence_x1_kernel(tc, h, xp, u, a, c1, c2, out_0
         def diag(b):
             for it in range(T):
                 d, off = dg[b % 2][it]
-                nc.vector.tensor_scalar(
-                    out=d[:, off : off + P], in0=ident[:], scalar1=dc2[:, it, b : b + 1], scalar2=None, op0=ALU.mult
+                nc.gpsimd.tensor_scalar(
+                    out=d[:, off : off + P], in0=ident[:], scalar1=dc2[:, it, b : b + 1], scalar2=0.0,
+                    op0=ALU.mult, op1=ALU.add,
                 )
 
-        def multiply(b):
-            acc[b] = []
-            for it in range(T):
+        def multiply(b, its):
+            for it in its:
                 ps = psum.tile([P, N], F32, name="mx%d" % it, tag="mx%d" % it)
                 nc.tensor.matmul_mx(
                     out=ps[:],
@@ -143,81 +151,125 @@ def tile_kroneckerfactoredrtrlinfluence_x1_kernel(tc, h, xp, u, a, c1, c2, out_0
                     start=True,
                     stop=True,
                 )
-                acc[b].append(ps)
+                acc[b, it] = ps
 
-        def empty(b):
-            o32[b] = outs.tile([P, T, N], F32, name="o32", align_bytes=64)
+        def empty(b, i0, i1):
+            if b not in o32:
+                o32[b] = outs.tile([P, T, N], F32, name="o32", align_bytes=64)
 
             def on_vector(it):
                 c0, cend = V_COLS[it]
                 nc.vector.scalar_tensor_tensor(
-                    out=o32[b][:, it, c0:cend], in0=acc[b][it][:, c0:cend], scalar=dc1[:, it, b : b + 1],
+                    out=o32[b][:, it, c0:cend], in0=acc[b, it][:, c0:cend], scalar=dc1[:, it, b : b + 1],
                     in1=dg[b % 2][it][0][:], op0=ALU.mult, op1=ALU.add,
                 )
 
             def on_scalar(it):
                 c0, cend = S_COLS[it]
                 nc.scalar.activation(
-                    out=o32[b][:, it, c0:cend], in_=acc[b][it][:, c0:cend], func=ACT.Copy, scale=dc1[:, it, b : b + 1]
+                    out=o32[b][:, it, c0:cend], in_=acc[b, it][:, c0:cend], func=ACT.Copy, scale=dc1[:, it, b : b + 1]
                 )
 
-            for i0, i1 in ((0, 1), (2, 3)):
-                on_vector(i0)
-                on_scalar(i1)
-                on_vector(i1)
-                on_scalar(i0)
+            on_vector(i0)
+            on_scalar(i1)
+            on_vector(i1)
+            on_scalar(i0)
 
-        def turn(b):
-            pbf[b] = stage.tile([P, N, T], BF16, name="pbf", align_bytes=64)
-            for it in range(T):
-                tp = psum.tile([P, T, P], F32, name="tp%d" % it, tag="tp%d" % it)
-                for t in range(T):
-                    nc.tensor.transpose(tp[:, t, :], o32[b][:, it, t:N:T], ident[:])
-                nc.scalar.copy(out=pbf[b][:, it * P : (it + 1) * P, :], in_=tp[:].rearrange("p t i -> p i t"))
+        def cast(b, its):
+            for it in its:
+                if it in WORDS:
+                    w = stage.tile([P, 2, P, 2], BF16, name="words%d" % it, align_bytes=64)
+                    nc.vector.tensor_copy(out=w[:], in_=o32[b][:, it, :].rearrange("p (q u e) -> p u q e", u=2, e=2))
+                    words[b, it] = w
 
-        def quantize_p(b):
+        def turn(b, its):
+            if b not in pbf:
+                pbf[b] = stage.tile([P, N, T], BF16, name="pbf", align_bytes=64)
+            for it in its:
+                dst = pbf[b][:, it * P : (it + 1) * P, :]
+                if it in WORDS:
+                    w = words.pop((b, it))[:].rearrange("p u q e -> p (u q e)").bitcast(F32)
+                    tp = psum.tile([P, 2, P], F32, name="tp%d" % it, tag="tp%d" % it)
+                    for v in range(2):
+                        nc.tensor.transpose(tp[:, v, :], w[:, v * P : (v + 1) * P], ident[:])
+                    dst = dst.rearrange("p i t -> p (i t)").bitcast(F32).rearrange("p (i v) -> p i v", v=2)
+                    src = tp[:].rearrange("p v i -> p i v")
+                else:
+                    tp = psum.tile([P, T, P], F32, name="tp%d" % it, tag="tp%d" % it)
+                    for t in range(T):
+                        nc.tensor.transpose(tp[:, t, :], o32[b][:, it, t:N:T], ident[:])
+                    src = tp[:].rearrange("p t i -> p i t")
+                if b == B - 1 and it in (0, 2):
+                    nc.vector.tensor_copy(out=dst, in_=src)
+                else:
+                    nc.scalar.copy(out=dst, in_=src)
+
+        def quantize_p(b, cols):
             g = b // GROUP
-            if b % GROUP == 0:
-                pscl[g] = keep.tile([P, GROUP * N], U8, name="pscl%d" % g, align_bytes=64)
-            pcodes[b] = stage.tile([P, N], U32, name="pcodes", align_bytes=64)
             k = b % GROUP
-            quantize(pbf.pop(b), pcodes[b][:], pscl[g][:, k * N : (k + 1) * N])
+            if b not in pcodes:
+                pcodes[b] = stage.tile([P, N], U32, name="pcodes", align_bytes=64)
+            if g not in pscl:
+                pscl[g] = keep.tile([P, GROUP * N], U8, name="pscl%d" % g, align_bytes=64)
+            quantize(pbf[b][:, cols, :], pcodes[b][:, cols], pscl[g][:, k * N + cols.start : k * N + cols.stop])
 
-        def store_o(b):
-            nc.sync.dma_start(out=out_0[b].rearrange("(t p) l -> p t l", p=P), in_=o32[b][:])
-
-        def store_p(b):
+        def store_o(b, its):
             nc.sync.dma_start(
-                out=out_1[0, :, b * N : (b + 1) * N, :].rearrange("p m t -> p (m t)").bitcast(I32),
-                in_=pcodes[b][:].bitcast(I32),
+                out=out_0[b].rearrange("(t p) l -> p t l", p=P)[:, its, :], in_=o32[b][:, its, :]
             )
-            if b % GROUP == GROUP - 1:
-                g = b // GROUP
-                for q in range(4):
-                    nc.sync.dma_start(
-                        out=out_2[0, 4 * q : 4 * q + 4, g * GROUP * N : (g + 1) * GROUP * N].bitcast(I32),
-                        in_=pscl[g][32 * q : 32 * q + 4, :].bitcast(I32),
-                    )
 
-        quantize_a(0)
+        def store_p(b, cols):
+            nc.sync.dma_start(
+                out=out_1[0, :, b * N + cols.start : b * N + cols.stop, :].rearrange("p m t -> p (m t)").bitcast(I32),
+                in_=pcodes[b][:, cols].bitcast(I32),
+            )
+
+        def store_scales(g):
+            for q in range(4):
+                nc.sync.dma_start(
+                    out=out_2[0, 4 * q : 4 * q + 4, g * GROUP * N : (g + 1) * GROUP * N].bitcast(I32),
+                    in_=pscl[g][32 * q : 32 * q + 4, :].bitcast(I32),
+                )
+
+        whole = slice(0, N)
         diag(0)
-        interleave_a(1)
-        for s in range(B + 2):
+        diag(1)
+        for s in range(B):
             if s + AHEAD < B:
                 load(s + AHEAD)
-            if s < B:
-                multiply(s)
-                empty(s)
-            if 1 <= s <= B:
-                turn(s - 1)
+            if s >= 1:
+                cast(s - 1, (2, 3))
+            multiply(s, (0, 1))
+            empty(s, 0, 1)
+            if s >= 1:
+                turn(s - 1, (0, 1))
+            multiply(s, (2, 3))
             if s + 1 < B:
                 quantize_a(s + 1)
-                diag(s + 1)
+            if s >= 2:
+                quantize_p(s - 2, whole)
+            empty(s, 2, 3)
+            if s >= 1:
+                turn(s - 1, (2, 3))
+            cast(s, (0, 1))
             if s + 2 < B:
                 interleave_a(s + 2)
+                diag(s + 2)
+            if s < B - 1:
+                store_o(s, slice(0, T))
+            else:
+                store_o(s, slice(0, 2))
+                store_o(s, slice(2, 4))
             if s >= 2:
-                quantize_p(s - 2)
-            if s < B:
-                store_o(s)
-            if s >= 2:
-                store_p(s - 2)
+                store_p(s - 2, whole)
+                if (s - 2) % GROUP == GROUP - 1:
+                    store_scales((s - 2) // GROUP)
+        cast(B - 1, (2, 3))
+        turn(B - 1, (0, 1))
+        quantize_p(B - 2, whole)
+        store_p(B - 2, whole)
+        turn(B - 1, (2, 3))
+        for cols in (slice(0, N // 2), slice(N // 2, N)):
+            quantize_p(B - 1, cols)
+            store_p(B - 1, cols)
+        store_scales(B // GROUP - 1)

@@ -17,13 +17,13 @@ P = 128
 T = 4
 FLOPS = 2 * B * N * N * N + 2 * B * N * N
 
-AHEAD = 8
+AHEAD = 15
 GROUP = 4
 
-V_COLS = ((0, 128), (0, 256), (256, 512), (384, 512))
-S_COLS = ((128, 512), (256, 512), (0, 256), (0, 384))
-WORDS = (1, 3)
-S_SHARE = 64
+V_COLS = ((0, 256), (0, 256), (256, 512), (384, 512))
+S_COLS = ((256, 512), (256, 512), (0, 256), (0, 384))
+WORDS = ()
+S_SHARE = 0
 S_SHARE_HEAD = 192
 
 
@@ -32,8 +32,8 @@ def tile_kroneckerfactoredrtrlinfluence_x1_kernel(tc, h, xp, u, a, c1, c2, out_0
     with ExitStack() as ctx:
         keep = ctx.enter_context(tc.tile_pool(name="keep", bufs=1))
         raws = ctx.enter_context(tc.tile_pool(name="raws", bufs=AHEAD + 1))
-        stage = ctx.enter_context(tc.tile_pool(name="stage", bufs=3))
-        outs = ctx.enter_context(tc.tile_pool(name="outs", bufs=5))
+        stage = ctx.enter_context(tc.tile_pool(name="stage", bufs=4))
+        outs = ctx.enter_context(tc.tile_pool(name="outs", bufs=6))
         psum = ctx.enter_context(tc.psum_pool(name="psum", bufs=1))
         ctx.enter_context(tc.manual_schedule())
 
@@ -44,7 +44,6 @@ def tile_kroneckerfactoredrtrlinfluence_x1_kernel(tc, h, xp, u, a, c1, c2, out_0
         nc.vector.memset(hz[:], 0.0)
         xz = keep.tile([P, N], BF16, name="xz", align_bytes=64)
         nc.gpsimd.memset(xz[:], 0.0)
-        nc.scalar.dma_start(out=hz[0:B, :], in_=h)
         u_raw = keep.tile([P, T, N], BF16, name="u_raw", align_bytes=64)
         nc.sync.dma_start(out=u_raw[:], in_=u.rearrange("(p j) i -> p j i", j=T))
 
@@ -52,6 +51,12 @@ def tile_kroneckerfactoredrtrlinfluence_x1_kernel(tc, h, xp, u, a, c1, c2, out_0
             raw[b] = raws.tile([P, T, N], BF16, name="a_raw", align_bytes=64)
             nc.sync.dma_start(out=raw[b][:], in_=a[b].rearrange("(p j) l -> p j l", j=T))
 
+        nc.sync.dma_start(out=hz[0:B, :], in_=h)
+        nc.sync.dma_start(out=xz[0:B, :], in_=xp)
+        c1t = keep.tile([P, B], BF16, name="c1t", align_bytes=64)
+        c2t = keep.tile([P, B], BF16, name="c2t", align_bytes=64)
+        nc.sync.dma_start(out=c1t[:], in_=c1.partition_broadcast(P))
+        nc.sync.dma_start(out=c2t[:], in_=c2.partition_broadcast(P))
         for b in range(AHEAD):
             load(b)
 
@@ -59,11 +64,6 @@ def tile_kroneckerfactoredrtrlinfluence_x1_kernel(tc, h, xp, u, a, c1, c2, out_0
         make_identity(nc, identb[:])
         ident = keep.tile([P, P], F32, name="ident")
         make_identity(nc, ident[:])
-        nc.scalar.dma_start(out=xz[0:B, :], in_=xp)
-        c1t = keep.tile([P, B], BF16, name="c1t", align_bytes=64)
-        c2t = keep.tile([P, B], BF16, name="c2t", align_bytes=64)
-        nc.scalar.dma_start(out=c1t[:], in_=c1.partition_broadcast(P))
-        nc.scalar.dma_start(out=c2t[:], in_=c2.partition_broadcast(P))
 
         dg = []
         for par in range(2):
@@ -82,6 +82,8 @@ def tile_kroneckerfactoredrtrlinfluence_x1_kernel(tc, h, xp, u, a, c1, c2, out_0
         def interleave(src, dst, share):
             cut = N - share
             for eng, cols in ((nc.vector.tensor_copy, slice(0, cut)), (nc.scalar.copy, slice(cut, N))):
+                if cols.start == cols.stop:
+                    continue
                 eng(
                     out=dst[:, cols, :].rearrange("p (c i) t -> p c t i", i=4),
                     in_=src[:, :, cols].rearrange("p t (c i) -> p c t i", i=4),
@@ -132,7 +134,7 @@ def tile_kroneckerfactoredrtrlinfluence_x1_kernel(tc, h, xp, u, a, c1, c2, out_0
             )
 
         def diag(b):
-            for it in range(T):
+            for it in reversed(range(T)):
                 d, off = dg[b % 2][it]
                 nc.gpsimd.tensor_scalar(
                     out=d[:, off : off + P], in0=ident[:], scalar1=dc2[:, it, b : b + 1], scalar2=0.0,
@@ -171,9 +173,9 @@ def tile_kroneckerfactoredrtrlinfluence_x1_kernel(tc, h, xp, u, a, c1, c2, out_0
                 )
 
             on_vector(i0)
-            on_scalar(i1)
             on_vector(i1)
             on_scalar(i0)
+            on_scalar(i1)
 
         def cast(b, its):
             for it in its:

from contextlib import ExitStack

import concourse.mybir as mybir
from concourse.masks import make_identity

F32 = mybir.dt.float32
BF16 = mybir.dt.bfloat16
U32 = mybir.dt.uint32
I32 = mybir.dt.int32
U8 = mybir.dt.uint8
FP8X4 = mybir.dt.float8_e4m3fn_x4
ALU = mybir.AluOpType
ACT = mybir.ActivationFunctionType

B, N = 16, 512
P = 128
T = 4
FLOPS = 2 * B * N * N * N + 2 * B * N * N

AHEAD = 15
GROUP = 4

V_COLS = ((0, 256), (0, 256), (256, 512), (384, 512))
S_COLS = ((256, 512), (256, 512), (0, 256), (0, 384))
WORDS = ()
S_SHARE = 0
S_SHARE_HEAD = 192


def tile_kroneckerfactoredrtrlinfluence_x1_kernel(tc, h, xp, u, a, c1, c2, out_0, out_1, out_2):
    nc = tc.nc
    with ExitStack() as ctx:
        keep = ctx.enter_context(tc.tile_pool(name="keep", bufs=1))
        raws = ctx.enter_context(tc.tile_pool(name="raws", bufs=AHEAD + 1))
        stage = ctx.enter_context(tc.tile_pool(name="stage", bufs=4))
        outs = ctx.enter_context(tc.tile_pool(name="outs", bufs=6))
        psum = ctx.enter_context(tc.psum_pool(name="psum", bufs=1))
        ctx.enter_context(tc.manual_schedule())

        raw, grp, codes, scl = {}, {}, {}, {}
        acc, o32, words, pbf, pcodes, pscl = {}, {}, {}, {}, {}, {}

        hz = keep.tile([P, N], BF16, name="hz", align_bytes=64)
        nc.vector.memset(hz[:], 0.0)
        xz = keep.tile([P, N], BF16, name="xz", align_bytes=64)
        nc.gpsimd.memset(xz[:], 0.0)
        u_raw = keep.tile([P, T, N], BF16, name="u_raw", align_bytes=64)
        nc.sync.dma_start(out=u_raw[:], in_=u.rearrange("(p j) i -> p j i", j=T))

        def load(b):
            raw[b] = raws.tile([P, T, N], BF16, name="a_raw", align_bytes=64)
            nc.sync.dma_start(out=raw[b][:], in_=a[b].rearrange("(p j) l -> p j l", j=T))

        nc.sync.dma_start(out=hz[0:B, :], in_=h)
        nc.sync.dma_start(out=xz[0:B, :], in_=xp)
        c1t = keep.tile([P, B], BF16, name="c1t", align_bytes=64)
        c2t = keep.tile([P, B], BF16, name="c2t", align_bytes=64)
        nc.sync.dma_start(out=c1t[:], in_=c1.partition_broadcast(P))
        nc.sync.dma_start(out=c2t[:], in_=c2.partition_broadcast(P))
        for b in range(AHEAD):
            load(b)

        identb = keep.tile([P, P], BF16, name="identb")
        make_identity(nc, identb[:])
        ident = keep.tile([P, P], F32, name="ident")
        make_identity(nc, ident[:])

        dg = []
        for par in range(2):
            tiles = []
            for it in range(T):
                w = V_COLS[it][1] - V_COLS[it][0]
                d = keep.tile([P, w], F32, name="dg%d%d" % (par, it), align_bytes=64)
                off = it * P - V_COLS[it][0]
                if off > 0:
                    nc.vector.memset(d[:, 0:off], 0.0)
                if off + P < w:
                    nc.vector.memset(d[:, off + P : w], 0.0)
                tiles.append((d, off))
            dg.append(tiles)

        def interleave(src, dst, share):
            cut = N - share
            for eng, cols in ((nc.vector.tensor_copy, slice(0, cut)), (nc.scalar.copy, slice(cut, N))):
                if cols.start == cols.stop:
                    continue
                eng(
                    out=dst[:, cols, :].rearrange("p (c i) t -> p c t i", i=4),
                    in_=src[:, :, cols].rearrange("p t (c i) -> p c t i", i=4),
                )

        def quantize(src, cw, sc):
            nc.vector.quantize_mx(out=cw.bitcast(FP8X4), scales=sc, in_=src.rearrange("p n t -> p (n t)"))

        u_grp = keep.tile([P, N, T], BF16, name="u_grp", align_bytes=64)
        u_codes = keep.tile([P, N], U32, name="u_codes", align_bytes=64)
        u_scl = keep.tile([P, N], U8, name="u_scl", align_bytes=64)

        def interleave_a(b, share=S_SHARE):
            grp[b] = stage.tile([P, N, T], BF16, name="a_grp", align_bytes=64)
            interleave(raw.pop(b), grp[b], share)

        def quantize_a(b):
            codes[b] = stage.tile([P, N], U32, name="a_codes", align_bytes=64)
            scl[b] = stage.tile([P, N], U8, name="a_scl", align_bytes=64)
            quantize(grp.pop(b)[:], codes[b][:], scl[b][:])

        hT_ps = psum.tile([P, T, P], BF16, name="hT_ps", tag="tp1")
        for j in range(T):
            nc.tensor.transpose(hT_ps[:, j, :], hz[:, j:N:T], identb[:])
        hT = keep.tile([P, T, B], BF16, name="hT", align_bytes=64)
        nc.scalar.copy(out=hT[:], in_=hT_ps[:, :, 0:B])
        z_ps = psum.tile([P, T, B], F32, name="z_ps", tag="tp0")
        for it in range(T):
            cols = slice(it * P, (it + 1) * P)
            nc.tensor.matmul(z_ps[:, it, :], lhsT=xz[:, cols], rhs=identb[:, 0:B], start=True, stop=False)
            for j in range(T):
                nc.tensor.matmul(z_ps[:, it, :], lhsT=u_raw[:, j, cols], rhs=hT[:, j, :], start=False, stop=(j == T - 1))
        interleave(u_raw, u_grp, S_SHARE_HEAD)
        interleave_a(0, S_SHARE_HEAD)
        th = keep.tile([P, T, B], F32, name="th", align_bytes=64)
        nc.scalar.activation(out=th[:], in_=z_ps[:], func=ACT.Tanh)
        quantize(u_grp[:], u_codes[:], u_scl[:])
        quantize_a(0)
        interleave_a(1)
        nth2 = keep.tile([P, T, B], F32, name="nth2", align_bytes=64)
        nc.vector.scalar_tensor_tensor(out=nth2[:], in0=th[:], scalar=-1.0, in1=th[:], op0=ALU.mult, op1=ALU.mult)
        dc1 = keep.tile([P, T, B], F32, name="dc1", align_bytes=64)
        dc2 = keep.tile([P, T, B], F32, name="dc2", align_bytes=64)
        for dst, c in ((dc2, c2t), (dc1, c1t)):
            nc.vector.scalar_tensor_tensor(
                out=dst[:], in0=nth2[:], scalar=1.0, in1=c[:].unsqueeze(1).to_broadcast([P, T, B]),
                op0=ALU.add, op1=ALU.mult,
            )

        def diag(b):
            for it in reversed(range(T)):
                d, off = dg[b % 2][it]
                nc.gpsimd.tensor_scalar(
                    out=d[:, off : off + P], in0=ident[:], scalar1=dc2[:, it, b : b + 1], scalar2=0.0,
                    op0=ALU.mult, op1=ALU.add,
                )

        def multiply(b, its):
            for it in its:
                ps = psum.tile([P, N], F32, name="mx%d" % it, tag="mx%d" % it)
                nc.tensor.matmul_mx(
                    out=ps[:],
                    lhsT=u_codes[:, it * P : (it + 1) * P].bitcast(FP8X4),
                    lhsT_scale=u_scl[:, it * P : (it + 1) * P],
                    rhs=codes[b][:].bitcast(FP8X4),
                    rhs_scale=scl[b][:],
                    start=True,
                    stop=True,
                )
                acc[b, it] = ps

        def empty(b, i0, i1):
            if b not in o32:
                o32[b] = outs.tile([P, T, N], F32, name="o32", align_bytes=64)

            def on_vector(it):
                c0, cend = V_COLS[it]
                nc.vector.scalar_tensor_tensor(
                    out=o32[b][:, it, c0:cend], in0=acc[b, it][:, c0:cend], scalar=dc1[:, it, b : b + 1],
                    in1=dg[b % 2][it][0][:], op0=ALU.mult, op1=ALU.add,
                )

            def on_scalar(it):
                c0, cend = S_COLS[it]
                nc.scalar.activation(
                    out=o32[b][:, it, c0:cend], in_=acc[b, it][:, c0:cend], func=ACT.Copy, scale=dc1[:, it, b : b + 1]
                )

            on_vector(i0)
            on_vector(i1)
            on_scalar(i0)
            on_scalar(i1)

        def cast(b, its):
            for it in its:
                if it in WORDS:
                    w = stage.tile([P, 2, P, 2], BF16, name="words%d" % it, align_bytes=64)
                    nc.vector.tensor_copy(out=w[:], in_=o32[b][:, it, :].rearrange("p (q u e) -> p u q e", u=2, e=2))
                    words[b, it] = w

        def turn(b, its):
            if b not in pbf:
                pbf[b] = stage.tile([P, N, T], BF16, name="pbf", align_bytes=64)
            for it in its:
                dst = pbf[b][:, it * P : (it + 1) * P, :]
                if it in WORDS:
                    w = words.pop((b, it))[:].rearrange("p u q e -> p (u q e)").bitcast(F32)
                    tp = psum.tile([P, 2, P], F32, name="tp%d" % it, tag="tp%d" % it)
                    for v in range(2):
                        nc.tensor.transpose(tp[:, v, :], w[:, v * P : (v + 1) * P], ident[:])
                    dst = dst.rearrange("p i t -> p (i t)").bitcast(F32).rearrange("p (i v) -> p i v", v=2)
                    src = tp[:].rearrange("p v i -> p i v")
                else:
                    tp = psum.tile([P, T, P], F32, name="tp%d" % it, tag="tp%d" % it)
                    for t in range(T):
                        nc.tensor.transpose(tp[:, t, :], o32[b][:, it, t:N:T], ident[:])
                    src = tp[:].rearrange("p t i -> p i t")
                if b == B - 1 and it in (0, 2):
                    nc.vector.tensor_copy(out=dst, in_=src)
                else:
                    nc.scalar.copy(out=dst, in_=src)

        def quantize_p(b, cols):
            g = b // GROUP
            k = b % GROUP
            if b not in pcodes:
                pcodes[b] = stage.tile([P, N], U32, name="pcodes", align_bytes=64)
            if g not in pscl:
                pscl[g] = keep.tile([P, GROUP * N], U8, name="pscl%d" % g, align_bytes=64)
            quantize(pbf[b][:, cols, :], pcodes[b][:, cols], pscl[g][:, k * N + cols.start : k * N + cols.stop])

        def store_o(b, its):
            nc.sync.dma_start(
                out=out_0[b].rearrange("(t p) l -> p t l", p=P)[:, its, :], in_=o32[b][:, its, :]
            )

        def store_p(b, cols):
            nc.sync.dma_start(
                out=out_1[0, :, b * N + cols.start : b * N + cols.stop, :].rearrange("p m t -> p (m t)").bitcast(I32),
                in_=pcodes[b][:, cols].bitcast(I32),
            )

        def store_scales(g):
            for q in range(4):
                nc.sync.dma_start(
                    out=out_2[0, 4 * q : 4 * q + 4, g * GROUP * N : (g + 1) * GROUP * N].bitcast(I32),
                    in_=pscl[g][32 * q : 32 * q + 4, :].bitcast(I32),
                )

        whole = slice(0, N)
        diag(0)
        diag(1)
        for s in range(B):
            if s + AHEAD < B:
                load(s + AHEAD)
            if s >= 1:
                cast(s - 1, (2, 3))
            multiply(s, (0, 1))
            empty(s, 0, 1)
            if s >= 1:
                turn(s - 1, (0, 1))
            multiply(s, (2, 3))
            if s + 1 < B:
                quantize_a(s + 1)
            if s >= 2:
                quantize_p(s - 2, whole)
            empty(s, 2, 3)
            if s >= 1:
                turn(s - 1, (2, 3))
            cast(s, (0, 1))
            if s + 2 < B:
                interleave_a(s + 2)
                diag(s + 2)
            if s < B - 1:
                store_o(s, slice(0, T))
            else:
                store_o(s, slice(0, 2))
                store_o(s, slice(2, 4))
            if s >= 2:
                store_p(s - 2, whole)
                if (s - 2) % GROUP == GROUP - 1:
                    store_scales((s - 2) // GROUP)
        cast(B - 1, (2, 3))
        turn(B - 1, (0, 1))
        quantize_p(B - 2, whole)
        store_p(B - 2, whole)
        turn(B - 1, (2, 3))
        for cols in (slice(0, N // 2), slice(N // 2, N)):
            quantize_p(B - 1, cols)
            store_p(B - 1, cols)
        store_scales(B // GROUP - 1)
